import numpy as np
import ml_dtypes


def mxq(x, axis, fmt="e4m3"):
    dtype, down = {"e4m3": (ml_dtypes.float8_e4m3fn, 7), "e5m2": (ml_dtypes.float8_e5m2, 14)}[fmt]
    v = np.moveaxis(np.asarray(x, np.float32).astype(ml_dtypes.bfloat16).astype(np.float64), axis, -1)
    blocks = v.reshape(v.shape[:-1] + (-1, 32))
    amax = np.abs(blocks).max(-1, keepdims=True)
    byte = np.maximum(np.where(amax > 0, np.frexp(amax)[1] - 1 + 127, 0) - down, 1)
    scale = np.exp2(byte - 127.0)
    codes = (blocks / scale).astype(np.float32).astype(dtype).astype(np.float64)
    return np.moveaxis((codes * scale).reshape(v.shape), -1, axis)


WIDE = False


def mx_kscale(k):
    if not WIDE:
        return np.ones(k)
    levels = np.array([10, -10, 5, -5, 0])
    if k % 512:
        return np.exp2(np.random.permutation(np.resize(levels, k // 32))).repeat(32)
    a = np.empty((k // 512, 16))
    for p in range(k // 512):
        a[p, :8] = np.random.permutation(np.resize(levels, 8))
        for g in range(8):
            far = levels[np.abs(levels - a[p, g]) >= 10]
            a[p, g + 8] = far[np.random.randint(len(far))]
    return np.exp2(a.ravel()).repeat(32)


def f64(x):
    return np.asarray(x).astype(np.float64)


def striped(idx):
    return np.tile(idx.reshape(-1, 16).T, (8, 1)).astype(np.uint16)


def unstriped(offs):
    return offs[:16].T.reshape(-1).astype(np.int64)


def relu(v):
    return np.maximum(v, 0.0)


K, T, E, C, H, N = 512, 1536, 12, 256, 512, 128


def by_expert(wq, xq):
    return np.concatenate([wq[e].T @ xq[:, e * C:(e + 1) * C] for e in range(E)], axis=1)


def setup_inputs():
    n = np.random.standard_normal
    s = mx_kscale(K)[:, None]
    u = mx_kscale(H)
    first = np.random.permutation(np.repeat(np.arange(E), T // E))
    second = (first + 1 + np.random.permutation(np.repeat(np.arange(E - 1), -(-T // (E - 1)))[:T])) % E
    while np.bincount(second, minlength=E).max() != T // E:
        load = np.bincount(second, minlength=E); hi, lo = int(load.argmax()), int(load.argmin())
        t = np.flatnonzero((second == hi) & (first != lo))[0]; second[t] = lo
    slot_token = np.empty(E * C, np.int64); pos = np.empty((2, T), np.int64); fill = np.zeros(E, np.int64)
    place = np.stack([np.random.permutation(C) for _ in range(E)])
    for r, deal in enumerate((first, second)):
        for t in np.random.permutation(T):
            e = deal[t]; j = e * C + place[e, fill[e]]; fill[e] += 1; slot_token[j] = t; pos[r, t] = j
    g = np.random.uniform(0.2, 0.8, T)
    return {
        "xT": (n((K, T)) * s).astype(np.float32),
        "w1": (n((E, K, H)) / np.sqrt(K) / s[None] * u[None, None, :]).astype(np.float32),
        "w2": (n((E, H, N)) / np.sqrt(H) / u[None, :, None]).astype(np.float32),
        "gate": np.stack([np.tile(g, (N, 1)), np.tile(1.0 - g, (N, 1))]).astype(np.float32),
        "offs": striped(slot_token),
        "pos1": striped(pos[0]),
        "pos2": striped(pos[1]),
    }


def reference(xT, w1, w2, gate, offs, pos1, pos2):
    idx = unstriped(offs)
    xq = mxq(f64(xT)[:, idx], 0, "e4m3")
    h = relu(by_expert(mxq(f64(w1), 1, "e4m3"), xq))
    y = by_expert(mxq(f64(w2), 1, "e4m3"), mxq(h, 0, "e4m3"))
    return f64(gate[0]) * y[:, unstriped(pos1)] + f64(gate[1]) * y[:, unstriped(pos2)]

@@ -1,0 +1,215 @@
+from contextlib import ExitStack
+
+import concourse.mybir as mybir
+
+K, T, E, C, H, N = 512, 1536, 12, 256, 512, 128
+P = 128
+PACK = 4
+SLOTS = E * C
+FLOPS = 2 * SLOTS * (K * H + H * N)
+
+F32 = mybir.dt.float32
+BF16 = mybir.dt.bfloat16
+U32 = mybir.dt.uint32
+U16 = mybir.dt.uint16
+U8 = mybir.dt.uint8
+FP8X4 = mybir.dt.float8_e4m3fn_x4
+MULT = mybir.AluOpType.mult
+RELU = mybir.ActivationFunctionType.Relu
+
+X_CHUNKS = ((0, 256, 160), (256, 256, 160), (512, 512, 320), (1024, 512, 320))
+GATHERS = {0: 1, 1: 1, 2: 2, 4: 2, 6: 2, 8: 2, 10: 2}
+W1_VECTOR = 56
+LAST_VECTOR = 80
+OUT_CHUNKS = ((0, 512), (512, 512), (1024, 256), (1280, 256))
+
+
+def interleave(copy, dst, src):
+    copy(
+        out=dst.rearrange("p (c i) j -> p c j i", i=4),
+        in_=src.rearrange("p j (c i) -> p c j i", i=4),
+    )
+
+
+def interleave_permuted(copy, dst, src, m0, m1):
+    copy(
+        out=dst[:, :, m0:m1, :].rearrange("p t m j -> p m j t"),
+        in_=src[:, :, 4 * m0 : 4 * m1].rearrange("p j (m t) -> p m j t", t=4),
+    )
+
+
+def tile_routed_moe_kernel(tc, xT, w1, w2, gate, offs, pos1, pos2, out):
+    nc = tc.nc
+    with ExitStack() as ctx:
+        keep = ctx.enter_context(tc.tile_pool(name="keep", bufs=1))
+        xin = ctx.enter_context(tc.tile_pool(name="xin", bufs=4))
+        win = ctx.enter_context(tc.tile_pool(name="win", bufs=6))
+        mid = ctx.enter_context(tc.tile_pool(name="mid", bufs=3))
+        wq = ctx.enter_context(tc.tile_pool(name="wq", bufs=4))
+        fin = ctx.enter_context(tc.tile_pool(name="fin", bufs=2))
+        hps = ctx.enter_context(tc.psum_pool(name="hps", bufs=5))
+        yps = ctx.enter_context(tc.psum_pool(name="yps", bufs=3))
+
+        offs_sb = keep.tile([P, SLOTS // 16], U16, name="offs_sb")
+        pos1_sb = keep.tile([P, T // 16], U16, name="pos1_sb")
+        pos2_sb = keep.tile([P, T // 16], U16, name="pos2_sb")
+        xq = keep.tile([P, T], U32, name="xq", align_bytes=64)
+        xs = keep.tile([P, T], U8, name="xs", align_bytes=64)
+        y_all = keep.tile([P, SLOTS], F32, name="y_all")
+        gate_sb = keep.tile([P, 2, T], F32, name="gate_sb")
+
+        nc.gpsimd.memset(xs[:], 0)
+
+        x_view = xT.rearrange("(p j) n -> p j n", j=PACK)
+        w2raws, w1raws, w2codes, w1codes, picks, hcodes = {}, {}, {}, {}, {}, {}
+
+        def tokens(c):
+            n0, width, cut = X_CHUNKS[c]
+            raw = xin.tile([P, PACK, width], F32, name="xraw", tag="xraw")
+            nc.sync.dma_start(out=raw[:], in_=x_view[:, :, n0 : n0 + width])
+            grouped = mid.tile([P, width, PACK], BF16, name="xg", tag="xg", align_bytes=64)
+            interleave(nc.vector.tensor_copy, grouped[:, :cut, :], raw[:, :, :cut])
+            interleave(nc.scalar.copy, grouped[:, cut:, :], raw[:, :, cut:])
+            nc.vector.quantize_mx(
+                out=xq[:, n0 : n0 + width].bitcast(FP8X4),
+                scales=xs[:, n0 : n0 + width],
+                in_=grouped[:].rearrange("p n j -> p (n j)"),
+            )
+
+        def load(e):
+            if e >= E:
+                return
+            w1raw = win.tile([P, PACK, H], F32, name="w1raw", tag="w1raw")
+            nc.sync.dma_start(out=w1raw[:], in_=w1[e].rearrange("(p j) c -> p j c", j=PACK))
+            w1raws[e] = w1raw
+            if e % 2 == 0:
+                w2raw = win.tile([P, 2, PACK, N], F32, name="w2raw", tag="w2raw", bufs=3)
+                nc.sync.dma_start(
+                    out=w2raw[:],
+                    in_=w2[e : e + 2].rearrange("e (p j) n -> p e j n", j=PACK),
+                )
+                w2raws[e] = w2raw
+
+        def weights1(e):
+            if e >= E:
+                return
+            w1raw = w1raws[e]
+            w1g = mid.tile([P, PACK, P, PACK], BF16, name="w1g", tag="w1g", align_bytes=64)
+            mv = LAST_VECTOR if e == E - 1 else W1_VECTOR
+            interleave_permuted(nc.vector.tensor_copy, w1g, w1raw, 0, mv)
+            interleave_permuted(nc.scalar.copy, w1g, w1raw, mv, P)
+            w1q = wq.tile([P, H], U32, name="w1q", tag="w1q", align_bytes=64)
+            w1s = wq.tile([P, H], U8, name="w1s", tag="w1s", align_bytes=64)
+            nc.vector.quantize_mx(
+                out=w1q[:].bitcast(FP8X4),
+                scales=w1s[:],
+                in_=w1g[:].rearrange("p t m j -> p (t m j)"),
+            )
+            w1codes[e] = (w1q, w1s)
+
+        def weights2(e):
+            if e >= E or e % 2:
+                return
+            w2raw = w2raws[e]
+            w2g = mid.tile([P, 2, N, PACK], BF16, name="w2g", tag="w2g", bufs=2, align_bytes=64)
+            for u in range(2):
+                interleave(nc.scalar.copy, w2g[:, u], w2raw[:, u])
+            w2q = wq.tile([P, 2 * N], U32, name="w2q", tag="w2q", align_bytes=64)
+            w2s = wq.tile([P, 2 * N], U8, name="w2s", tag="w2s", align_bytes=64)
+            nc.vector.quantize_mx(
+                out=w2q[:].bitcast(FP8X4),
+                scales=w2s[:],
+                in_=w2g[:].rearrange("p e n j -> p (e n j)"),
+            )
+            w2codes[e] = (w2q, w2s)
+
+        def gather(e):
+            if e not in GATHERS:
+                return
+            s0, s1 = e * C, (e + GATHERS[e]) * C
+            picked = offs_sb[:, s0 // 16 : s1 // 16]
+            gq = wq.tile([P, s1 - s0], U32, name="gq", tag="gq", bufs=2, align_bytes=64)
+            gs = wq.tile([P, s1 - s0], U8, name="gs", tag="gs", bufs=2, align_bytes=64)
+            nc.vector.tensor_copy(out=gq[:], in_=xq[:].indirect(picked))
+            nc.vector.tensor_copy(out=gs[:], in_=xs[:].indirect(picked))
+            for f in range(e, e + GATHERS[e]):
+                picks[f] = (gq, gs, (f - e) * C)
+
+        def layer1(e):
+            w1q, w1s = w1codes[e]
+            gq, gs, base = picks[e]
+            hg = mid.tile([P, C, PACK], BF16, name="hg", tag="hg", align_bytes=64)
+            for half in range(2):
+                n0 = base + half * P
+                hp = hps.tile([P, PACK, P], F32, name="hp", tag="hp")
+                for t in range(PACK):
+                    nc.tensor.matmul_mx(
+                        out=hp[:, t, :],
+                        lhsT=w1q[:, t * P : (t + 1) * P].bitcast(FP8X4),
+                        lhsT_scale=w1s[:, t * P : (t + 1) * P],
+                        rhs=gq[:, n0 : n0 + P].bitcast(FP8X4),
+                        rhs_scale=gs[:, n0 : n0 + P],
+                        start=True,
+                        stop=True,
+                    )
+                nc.scalar.activation(
+                    out=hg[:, half * P : (half + 1) * P, :],
+                    in_=hp[:].rearrange("p t n -> p n t"),
+                    func=RELU,
+                )
+            hcodes[e] = hg
+
+        def layer2(e):
+            hg = hcodes[e]
+            hq = wq.tile([P, C], U32, name="hq", tag="hq", align_bytes=64)
+            hs = wq.tile([P, C], U8, name="hs", tag="hs", align_bytes=64)
+            nc.vector.quantize_mx(
+                out=hq[:].bitcast(FP8X4),
+                scales=hs[:],
+                in_=hg[:].rearrange("p n t -> p (n t)"),
+            )
+            yp = yps.tile([P, C], F32, name="yp", tag="yp")
+            u = e % 2
+            w2q, w2s = w2codes[e - u]
+            nc.tensor.matmul_mx(
+                out=yp[:],
+                lhsT=w2q[:, u * N : (u + 1) * N].bitcast(FP8X4),
+                lhsT_scale=w2s[:, u * N : (u + 1) * N],
+                rhs=hq[:].bitcast(FP8X4),
+                rhs_scale=hs[:],
+                start=True,
+                stop=True,
+            )
+            nc.scalar.copy(out=y_all[:, e * C : (e + 1) * C], in_=yp[:])
+
+        tokens(0)
+        tokens(1)
+        nc.sync.dma_start(offs_sb[:], offs)
+        tokens(2)
+        tokens(3)
+        for e in range(E):
+            load(e)
+            weights2(e)
+            weights1(e)
+            gather(e)
+            layer1(e)
+            layer2(e)
+
+        nc.sync.dma_start(pos1_sb[:], pos1)
+        nc.sync.dma_start(pos2_sb[:], pos2)
+        nc.sync.dma_start(out=gate_sb[:], in_=gate.rearrange("g p t -> p g t"))
+
+        for t0, width in OUT_CHUNKS:
+            parts = []
+            for r, pos in ((0, pos1_sb), (1, pos2_sb)):
+                part = fin.tile([P, width], F32, name="part", tag=f"part{r}")
+                nc.vector.tensor_tensor(
+                    out=part[:],
+                    in0=y_all[:].indirect(pos[:, t0 // 16 : (t0 + width) // 16]),
+                    in1=gate_sb[:, r, t0 : t0 + width],
+                    op=MULT,
+                )
+                parts.append(part)
+            total = fin.tile([P, width], F32, name="total", tag="total")
+            nc.vector.tensor_add(out=total[:], in0=parts[0][:], in1=parts[1][:])
+            nc.sync.dma_start(out=out[:, t0 : t0 + width], in_=total[:])

@@ -15,13 +15,17 @@ U16 = mybir.dt.uint16
 U8 = mybir.dt.uint8
 FP8X4 = mybir.dt.float8_e4m3fn_x4
 MULT = mybir.AluOpType.mult
+ADD = mybir.AluOpType.add
 RELU = mybir.ActivationFunctionType.Relu
 
 X_CHUNKS = ((0, 256, 160), (256, 256, 160), (512, 512, 320), (1024, 512, 320))
-GATHERS = {0: 1, 1: 1, 2: 2, 4: 2, 6: 2, 8: 2, 10: 2}
-W1_VECTOR = 56
+W1_VECTOR = 44
 LAST_VECTOR = 80
-OUT_CHUNKS = ((0, 512), (512, 512), (1024, 256), (1280, 256))
+OUT_CHUNKS = ((0, 640), (640, 576), (1216, 320))
+RING = 7
+SLOT = PACK * H * 4
+AT_HG, AT_HQ, AT_HS, AT_GQ, AT_GS = 0, 2048, 3072, 3328, 4352
+GROUPED = PACK * H * 2
 
 
 def interleave(copy, dst, src):
@@ -42,9 +46,10 @@ def tile_routed_moe_kernel(tc, xT, w1, w2, gate, offs, pos1, pos2, out):
     nc = tc.nc
     with ExitStack() as ctx:
         keep = ctx.enter_context(tc.tile_pool(name="keep", bufs=1))
+        ring = ctx.enter_context(tc.tile_pool(name="ring", bufs=1))
+        mid = ctx.enter_context(tc.tile_pool(name="mid", bufs=1))
         xin = ctx.enter_context(tc.tile_pool(name="xin", bufs=4))
-        win = ctx.enter_context(tc.tile_pool(name="win", bufs=6))
-        mid = ctx.enter_context(tc.tile_pool(name="mid", bufs=3))
+        win = ctx.enter_context(tc.tile_pool(name="win", bufs=3))
         wq = ctx.enter_context(tc.tile_pool(name="wq", bufs=4))
         fin = ctx.enter_context(tc.tile_pool(name="fin", bufs=2))
         hps = ctx.enter_context(tc.psum_pool(name="hps", bufs=5))
@@ -61,15 +66,24 @@ def tile_routed_moe_kernel(tc, xT, w1, w2, gate, offs, pos1, pos2, out):
         nc.gpsimd.memset(xs[:], 0)
 
         x_view = xT.rearrange("(p j) n -> p j n", j=PACK)
-        w2raws, w1raws, w2codes, w1codes, picks, hcodes = {}, {}, {}, {}, {}, {}
+        w2raws, w1raws, w1gs, w2codes, w1codes, picks, hgs = {}, {}, {}, {}, {}, {}, {}
+
+        def in_ring(shape, dtype, name, stage, at):
+            if stage is None:
+                return keep.tile(shape, dtype, name=name, align_bytes=64)
+            return ring.tile(shape, dtype, name=name, align_bytes=64, offset=(stage % RING) * SLOT + at)
+
+        def in_mid(shape, name, stage):
+            return mid.tile(shape, BF16, name=name, align_bytes=64, offset=(stage % 3) * GROUPED)
 
         def tokens(c):
             n0, width, cut = X_CHUNKS[c]
             raw = xin.tile([P, PACK, width], F32, name="xraw", tag="xraw")
             nc.sync.dma_start(out=raw[:], in_=x_view[:, :, n0 : n0 + width])
-            grouped = mid.tile([P, width, PACK], BF16, name="xg", tag="xg", align_bytes=64)
+            grouped = xin.tile([P, width, PACK], BF16, name="xg", tag="xg", align_bytes=64)
             interleave(nc.vector.tensor_copy, grouped[:, :cut, :], raw[:, :, :cut])
-            interleave(nc.scalar.copy, grouped[:, cut:, :], raw[:, :, cut:])
+            if cut < width:
+                interleave(nc.scalar.copy, grouped[:, cut:, :], raw[:, :, cut:])
             nc.vector.quantize_mx(
                 out=xq[:, n0 : n0 + width].bitcast(FP8X4),
                 scales=xs[:, n0 : n0 + width],
@@ -79,68 +93,72 @@ def tile_routed_moe_kernel(tc, xT, w1, w2, gate, offs, pos1, pos2, out):
         def load(e):
             if e >= E:
                 return
-            w1raw = win.tile([P, PACK, H], F32, name="w1raw", tag="w1raw")
+            w1raw = in_ring([P, PACK, H], F32, f"w1raw{e}", e, 0)
             nc.sync.dma_start(out=w1raw[:], in_=w1[e].rearrange("(p j) c -> p j c", j=PACK))
             w1raws[e] = w1raw
-            if e % 2 == 0:
-                w2raw = win.tile([P, 2, PACK, N], F32, name="w2raw", tag="w2raw", bufs=3)
+            if e % 2 == 1:
+                w2raw = win.tile([P, 2, PACK, N], F32, name="w2raw", tag="w2raw")
                 nc.sync.dma_start(
                     out=w2raw[:],
-                    in_=w2[e : e + 2].rearrange("e (p j) n -> p e j n", j=PACK),
+                    in_=w2[e - 1 : e + 1].rearrange("e (p j) n -> p e j n", j=PACK),
                 )
-                w2raws[e] = w2raw
+                w2raws[e - 1] = w2raw[:, 0]
+                w2raws[e] = w2raw[:, 1]
 
-        def weights1(e):
-            if e >= E:
-                return
+        def group1(e):
             w1raw = w1raws[e]
-            w1g = mid.tile([P, PACK, P, PACK], BF16, name="w1g", tag="w1g", align_bytes=64)
+            w1g = in_mid([P, PACK, P, PACK], f"w1g{e}", e)
             mv = LAST_VECTOR if e == E - 1 else W1_VECTOR
             interleave_permuted(nc.vector.tensor_copy, w1g, w1raw, 0, mv)
             interleave_permuted(nc.scalar.copy, w1g, w1raw, mv, P)
+            w1gs[e] = w1g
+
+        def quantise1(e):
             w1q = wq.tile([P, H], U32, name="w1q", tag="w1q", align_bytes=64)
             w1s = wq.tile([P, H], U8, name="w1s", tag="w1s", align_bytes=64)
             nc.vector.quantize_mx(
                 out=w1q[:].bitcast(FP8X4),
                 scales=w1s[:],
-                in_=w1g[:].rearrange("p t m j -> p (t m j)"),
+                in_=w1gs[e][:].rearrange("p t m j -> p (t m j)"),
             )
             w1codes[e] = (w1q, w1s)
 
-        def weights2(e):
-            if e >= E or e % 2:
-                return
+        def weights2(e, stage):
             w2raw = w2raws[e]
-            w2g = mid.tile([P, 2, N, PACK], BF16, name="w2g", tag="w2g", bufs=2, align_bytes=64)
-            for u in range(2):
-                interleave(nc.scalar.copy, w2g[:, u], w2raw[:, u])
-            w2q = wq.tile([P, 2 * N], U32, name="w2q", tag="w2q", align_bytes=64)
-            w2s = wq.tile([P, 2 * N], U8, name="w2s", tag="w2s", align_bytes=64)
+            w2g = in_mid([P, N, PACK], f"w2g{e}", stage)
+            nc.gpsimd.tensor_scalar(
+                out=w2g.rearrange("p (c i) j -> p c j i", i=4),
+                in0=w2raw.rearrange("p j (c i) -> p c j i", i=4),
+                scalar1=1.0,
+                scalar2=0.0,
+                op0=MULT,
+                op1=ADD,
+            )
+            w2q = wq.tile([P, N], U32, name="w2q", tag="w2q", align_bytes=64)
+            w2s = wq.tile([P, N], U8, name="w2s", tag="w2s", align_bytes=64)
             nc.vector.quantize_mx(
                 out=w2q[:].bitcast(FP8X4),
                 scales=w2s[:],
-                in_=w2g[:].rearrange("p e n j -> p (e n j)"),
+                in_=w2g[:].rearrange("p n j -> p (n j)"),
             )
             w2codes[e] = (w2q, w2s)
 
-        def gather(e):
-            if e not in GATHERS:
+        def gather(e, stage):
+            if e >= E:
                 return
-            s0, s1 = e * C, (e + GATHERS[e]) * C
-            picked = offs_sb[:, s0 // 16 : s1 // 16]
-            gq = wq.tile([P, s1 - s0], U32, name="gq", tag="gq", bufs=2, align_bytes=64)
-            gs = wq.tile([P, s1 - s0], U8, name="gs", tag="gs", bufs=2, align_bytes=64)
+            picked = offs_sb[:, e * C // 16 : (e + 1) * C // 16]
+            gq = in_ring([P, C], U32, f"gq{e}", stage, AT_GQ)
+            gs = in_ring([P, C], U8, f"gs{e}", stage, AT_GS)
             nc.vector.tensor_copy(out=gq[:], in_=xq[:].indirect(picked))
             nc.vector.tensor_copy(out=gs[:], in_=xs[:].indirect(picked))
-            for f in range(e, e + GATHERS[e]):
-                picks[f] = (gq, gs, (f - e) * C)
+            picks[e] = (gq, gs)
 
-        def layer1(e):
+        def layer1(e, stage):
             w1q, w1s = w1codes[e]
-            gq, gs, base = picks[e]
-            hg = mid.tile([P, C, PACK], BF16, name="hg", tag="hg", align_bytes=64)
+            gq, gs = picks[e]
+            hg = in_ring([P, C, PACK], BF16, f"hg{e}", stage, AT_HG)
             for half in range(2):
-                n0 = base + half * P
+                n0 = half * P
                 hp = hps.tile([P, PACK, P], F32, name="hp", tag="hp")
                 for t in range(PACK):
                     nc.tensor.matmul_mx(
@@ -157,24 +175,22 @@ def tile_routed_moe_kernel(tc, xT, w1, w2, gate, offs, pos1, pos2, out):
                     in_=hp[:].rearrange("p t n -> p n t"),
                     func=RELU,
                 )
-            hcodes[e] = hg
+            hgs[e] = hg
 
-        def layer2(e):
-            hg = hcodes[e]
-            hq = wq.tile([P, C], U32, name="hq", tag="hq", align_bytes=64)
-            hs = wq.tile([P, C], U8, name="hs", tag="hs", align_bytes=64)
+        def layer2(e, stage):
+            hq = in_ring([P, C], U32, f"hq{e}", stage, AT_HQ)
+            hs = in_ring([P, C], U8, f"hs{e}", stage, AT_HS)
             nc.vector.quantize_mx(
                 out=hq[:].bitcast(FP8X4),
                 scales=hs[:],
-                in_=hg[:].rearrange("p n t -> p (n t)"),
+                in_=hgs[e][:].rearrange("p n t -> p (n t)"),
             )
             yp = yps.tile([P, C], F32, name="yp", tag="yp")
-            u = e % 2
-            w2q, w2s = w2codes[e - u]
+            w2q, w2s = w2codes[e]
             nc.tensor.matmul_mx(
                 out=yp[:],
-                lhsT=w2q[:, u * N : (u + 1) * N].bitcast(FP8X4),
-                lhsT_scale=w2s[:, u * N : (u + 1) * N],
+                lhsT=w2q[:].bitcast(FP8X4),
+                lhsT_scale=w2s[:],
                 rhs=hq[:].bitcast(FP8X4),
                 rhs_scale=hs[:],
                 start=True,
@@ -185,15 +201,26 @@ def tile_routed_moe_kernel(tc, xT, w1, w2, gate, offs, pos1, pos2, out):
         tokens(0)
         tokens(1)
         nc.sync.dma_start(offs_sb[:], offs)
-        tokens(2)
-        tokens(3)
-        for e in range(E):
+        for c in range(2, len(X_CHUNKS)):
+            tokens(c)
+        for e in range(RING):
             load(e)
-            weights2(e)
-            weights1(e)
-            gather(e)
-            layer1(e)
-            layer2(e)
+        gather(0, None)
+        for e in range(E):
+            group1(e)
+            if e >= 1:
+                layer1(e - 1, e)
+            if e >= 2:
+                layer2(e - 2, e)
+                load(e + RING - 2)
+            quantise1(e)
+            gather(e + 1, e)
+            if e >= 1:
+                weights2(e - 1, e)
+        weights2(E - 1, E)
+        layer1(E - 1, None)
+        layer2(E - 2, None)
+        layer2(E - 1, None)
 
         nc.sync.dma_start(pos1_sb[:], pos1)
         nc.sync.dma_start(pos2_sb[:], pos2)

@@ -18,13 +18,15 @@ MULT = mybir.AluOpType.mult
 ADD = mybir.AluOpType.add
 RELU = mybir.ActivationFunctionType.Relu
 
-X_CHUNKS = ((0, 256, 160), (256, 256, 160), (512, 512, 320), (1024, 512, 320))
+X_CHUNKS = ((0, 512, 320), (512, 512, 320), (1024, 256, 160), (1280, 256, 160))
 W1_VECTOR = 44
-LAST_VECTOR = 80
+LAST_VECTOR = 56
+W1_GPSIMD = 24
+VECTOR_RELU = ((11, 1),)
 OUT_CHUNKS = ((0, 640), (640, 576), (1216, 320))
-RING = 7
+RING = 8
 SLOT = PACK * H * 4
-AT_HG, AT_HQ, AT_HS, AT_GQ, AT_GS = 0, 2048, 3072, 3328, 4352
+AT_HG, AT_HQ, AT_HS, AT_GQ, AT_GS = 0, 2048, 3072, 3328, 5376
 GROUPED = PACK * H * 2
 
 
@@ -66,7 +68,10 @@ def tile_routed_moe_kernel(tc, xT, w1, w2, gate, offs, pos1, pos2, out):
         nc.gpsimd.memset(xs[:], 0)
 
         x_view = xT.rearrange("(p j) n -> p j n", j=PACK)
-        w2raws, w1raws, w1gs, w2codes, w1codes, picks, hgs = {}, {}, {}, {}, {}, {}, {}
+        w2raws, w1raws, w1gs, w2codes, w1codes, words, scales, hgs = {}, {}, {}, {}, {}, {}, {}, {}
+
+        def gpsimd_copy(out, in_):
+            nc.gpsimd.tensor_scalar(out=out, in0=in_, scalar1=1.0, scalar2=0.0, op0=MULT, op1=ADD)
 
         def in_ring(shape, dtype, name, stage, at):
             if stage is None:
@@ -110,7 +115,10 @@ def tile_routed_moe_kernel(tc, xT, w1, w2, gate, offs, pos1, pos2, out):
             w1g = in_mid([P, PACK, P, PACK], f"w1g{e}", e)
             mv = LAST_VECTOR if e == E - 1 else W1_VECTOR
             interleave_permuted(nc.vector.tensor_copy, w1g, w1raw, 0, mv)
-            interleave_permuted(nc.scalar.copy, w1g, w1raw, mv, P)
+            mg = W1_GPSIMD if e >= 1 else 0
+            if mg:
+                interleave_permuted(gpsimd_copy, w1g, w1raw, mv, mv + mg)
+            interleave_permuted(nc.scalar.copy, w1g, w1raw, mv + mg, P)
             w1gs[e] = w1g
 
         def quantise1(e):
@@ -126,14 +134,7 @@ def tile_routed_moe_kernel(tc, xT, w1, w2, gate, offs, pos1, pos2, out):
         def weights2(e, stage):
             w2raw = w2raws[e]
             w2g = in_mid([P, N, PACK], f"w2g{e}", stage)
-            nc.gpsimd.tensor_scalar(
-                out=w2g.rearrange("p (c i) j -> p c j i", i=4),
-                in0=w2raw.rearrange("p j (c i) -> p c j i", i=4),
-                scalar1=1.0,
-                scalar2=0.0,
-                op0=MULT,
-                op1=ADD,
-            )
+            interleave(gpsimd_copy, w2g, w2raw)
             w2q = wq.tile([P, N], U32, name="w2q", tag="w2q", align_bytes=64)
             w2s = wq.tile([P, N], U8, name="w2s", tag="w2s", align_bytes=64)
             nc.vector.quantize_mx(
@@ -143,22 +144,25 @@ def tile_routed_moe_kernel(tc, xT, w1, w2, gate, offs, pos1, pos2, out):
             )
             w2codes[e] = (w2q, w2s)
 
-        def gather(e, stage):
+        def gather(sort, e, stage):
             if e >= E:
                 return
-            picked = offs_sb[:, e * C // 16 : (e + 1) * C // 16]
-            gq = in_ring([P, C], U32, f"gq{e}", stage, AT_GQ)
-            gs = in_ring([P, C], U8, f"gs{e}", stage, AT_GS)
-            nc.vector.tensor_copy(out=gq[:], in_=xq[:].indirect(picked))
-            nc.vector.tensor_copy(out=gs[:], in_=xs[:].indirect(picked))
-            picks[e] = (gq, gs)
+            picked = offs_sb[:, e * C // 16 : (e + 2) * C // 16]
+            if sort == 0:
+                gq = in_ring([P, 2 * C], U32, f"gq{e}", stage, AT_GQ)
+                nc.vector.tensor_copy(out=gq[:], in_=xq[:].indirect(picked))
+                words[e] = gq
+            else:
+                gs = in_ring([P, 2 * C], U8, f"gs{e}", stage, AT_GS)
+                nc.vector.tensor_copy(out=gs[:], in_=xs[:].indirect(picked))
+                scales[e] = gs
 
         def layer1(e, stage):
             w1q, w1s = w1codes[e]
-            gq, gs = picks[e]
+            gq, gs = words[e - e % 2], scales[e - e % 2]
             hg = in_ring([P, C, PACK], BF16, f"hg{e}", stage, AT_HG)
             for half in range(2):
-                n0 = half * P
+                n0 = e % 2 * C + half * P
                 hp = hps.tile([P, PACK, P], F32, name="hp", tag="hp")
                 for t in range(PACK):
                     nc.tensor.matmul_mx(
@@ -170,11 +174,12 @@ def tile_routed_moe_kernel(tc, xT, w1, w2, gate, offs, pos1, pos2, out):
                         start=True,
                         stop=True,
                     )
-                nc.scalar.activation(
-                    out=hg[:, half * P : (half + 1) * P, :],
-                    in_=hp[:].rearrange("p t n -> p n t"),
-                    func=RELU,
-                )
+                hidden = hg[:, half * P : (half + 1) * P, :]
+                sums = hp[:].rearrange("p t n -> p n t")
+                if (e, half) in VECTOR_RELU:
+                    nc.vector.tensor_scalar_max(hidden, sums, 0.0)
+                else:
+                    nc.scalar.activation(out=hidden, in_=sums, func=RELU)
             hgs[e] = hg
 
         def layer2(e, stage):
@@ -205,16 +210,18 @@ def tile_routed_moe_kernel(tc, xT, w1, w2, gate, offs, pos1, pos2, out):
             tokens(c)
         for e in range(RING):
             load(e)
-        gather(0, None)
+        gather(0, 0, None)
+        gather(1, 0, None)
         for e in range(E):
             group1(e)
             if e >= 1:
                 layer1(e - 1, e)
             if e >= 2:
                 layer2(e - 2, e)
-                load(e + RING - 2)
+            if e >= 4:
+                load(e + RING - 4)
             quantise1(e)
-            gather(e + 1, e)
+            gather(e % 2, e + 2 - e % 2, e)
             if e >= 1:
                 weights2(e - 1, e)
         weights2(E - 1, E)

@@ -19,11 +19,10 @@ ADD = mybir.AluOpType.add
 RELU = mybir.ActivationFunctionType.Relu
 
 X_CHUNKS = ((0, 512, 320), (512, 512, 320), (1024, 256, 160), (1280, 256, 160))
-W1_VECTOR = 44
-LAST_VECTOR = 56
-W1_GPSIMD = 24
+W1_VECTOR = 52
+LAST_VECTOR = 80
 VECTOR_RELU = ((11, 1),)
-OUT_CHUNKS = ((0, 640), (640, 576), (1216, 320))
+OUT_CHUNKS = ((0, 704), (704, 576), (1280, 256))
 RING = 8
 SLOT = PACK * H * 4
 AT_HG, AT_HQ, AT_HS, AT_GQ, AT_GS = 0, 2048, 3072, 3328, 5376
@@ -70,9 +69,6 @@ def tile_routed_moe_kernel(tc, xT, w1, w2, gate, offs, pos1, pos2, out):
         x_view = xT.rearrange("(p j) n -> p j n", j=PACK)
         w2raws, w1raws, w1gs, w2codes, w1codes, words, scales, hgs = {}, {}, {}, {}, {}, {}, {}, {}
 
-        def gpsimd_copy(out, in_):
-            nc.gpsimd.tensor_scalar(out=out, in0=in_, scalar1=1.0, scalar2=0.0, op0=MULT, op1=ADD)
-
         def in_ring(shape, dtype, name, stage, at):
             if stage is None:
                 return keep.tile(shape, dtype, name=name, align_bytes=64)
@@ -115,10 +111,7 @@ def tile_routed_moe_kernel(tc, xT, w1, w2, gate, offs, pos1, pos2, out):
             w1g = in_mid([P, PACK, P, PACK], f"w1g{e}", e)
             mv = LAST_VECTOR if e == E - 1 else W1_VECTOR
             interleave_permuted(nc.vector.tensor_copy, w1g, w1raw, 0, mv)
-            mg = W1_GPSIMD if e >= 1 else 0
-            if mg:
-                interleave_permuted(gpsimd_copy, w1g, w1raw, mv, mv + mg)
-            interleave_permuted(nc.scalar.copy, w1g, w1raw, mv + mg, P)
+            interleave_permuted(nc.scalar.copy, w1g, w1raw, mv, P)
             w1gs[e] = w1g
 
         def quantise1(e):
@@ -134,7 +127,14 @@ def tile_routed_moe_kernel(tc, xT, w1, w2, gate, offs, pos1, pos2, out):
         def weights2(e, stage):
             w2raw = w2raws[e]
             w2g = in_mid([P, N, PACK], f"w2g{e}", stage)
-            interleave(gpsimd_copy, w2g, w2raw)
+            nc.gpsimd.tensor_scalar(
+                out=w2g[:],
+                in0=w2raw.rearrange("p j n -> p n j"),
+                scalar1=1.0,
+                scalar2=0.0,
+                op0=MULT,
+                op1=ADD,
+            )
             w2q = wq.tile([P, N], U32, name="w2q", tag="w2q", align_bytes=64)
             w2s = wq.tile([P, N], U8, name="w2s", tag="w2s", align_bytes=64)
             nc.vector.quantize_mx(
@@ -233,7 +233,8 @@ def tile_routed_moe_kernel(tc, xT, w1, w2, gate, offs, pos1, pos2, out):
         nc.sync.dma_start(pos2_sb[:], pos2)
         nc.sync.dma_start(out=gate_sb[:], in_=gate.rearrange("g p t -> p g t"))
 
-        for t0, width in OUT_CHUNKS:
+        def fetch(c):
+            t0, width = OUT_CHUNKS[c]
             parts = []
             for r, pos in ((0, pos1_sb), (1, pos2_sb)):
                 part = fin.tile([P, width], F32, name="part", tag=f"part{r}")
@@ -244,6 +245,17 @@ def tile_routed_moe_kernel(tc, xT, w1, w2, gate, offs, pos1, pos2, out):
                     op=MULT,
                 )
                 parts.append(part)
+            return parts
+
+        def finish(c, parts):
+            t0, width = OUT_CHUNKS[c]
             total = fin.tile([P, width], F32, name="total", tag="total")
             nc.vector.tensor_add(out=total[:], in0=parts[0][:], in1=parts[1][:])
             nc.sync.dma_start(out=out[:, t0 : t0 + width], in_=total[:])
+
+        fetched = fetch(0)
+        for c in range(1, len(OUT_CHUNKS)):
+            following = fetch(c)
+            finish(c - 1, fetched)
+            fetched = following
+        finish(len(OUT_CHUNKS) - 1, fetched)

@@ -15,14 +15,13 @@ U16 = mybir.dt.uint16
 U8 = mybir.dt.uint8
 FP8X4 = mybir.dt.float8_e4m3fn_x4
 MULT = mybir.AluOpType.mult
-ADD = mybir.AluOpType.add
 RELU = mybir.ActivationFunctionType.Relu
 
 X_CHUNKS = ((0, 512, 320), (512, 512, 320), (1024, 256, 160), (1280, 256, 160))
-W1_VECTOR = 52
-LAST_VECTOR = 80
+W1_VECTOR = (40, 48)
+LAST_VECTOR = 72
 VECTOR_RELU = ((11, 1),)
-OUT_CHUNKS = ((0, 704), (704, 576), (1280, 256))
+OUT_CHUNKS = ((0, 640), (640, 576), (1216, 320))
 RING = 8
 SLOT = PACK * H * 4
 AT_HG, AT_HQ, AT_HS, AT_GQ, AT_GS = 0, 2048, 3072, 3328, 5376
@@ -67,7 +66,7 @@ def tile_routed_moe_kernel(tc, xT, w1, w2, gate, offs, pos1, pos2, out):
         nc.gpsimd.memset(xs[:], 0)
 
         x_view = xT.rearrange("(p j) n -> p j n", j=PACK)
-        w2raws, w1raws, w1gs, w2codes, w1codes, words, scales, hgs = {}, {}, {}, {}, {}, {}, {}, {}
+        w2raws, w1raws, w1gs, w2codes, w1codes, words, scales, hgs, w2gs = {}, {}, {}, {}, {}, {}, {}, {}, {}
 
         def in_ring(shape, dtype, name, stage, at):
             if stage is None:
@@ -109,7 +108,7 @@ def tile_routed_moe_kernel(tc, xT, w1, w2, gate, offs, pos1, pos2, out):
         def group1(e):
             w1raw = w1raws[e]
             w1g = in_mid([P, PACK, P, PACK], f"w1g{e}", e)
-            mv = LAST_VECTOR if e == E - 1 else W1_VECTOR
+            mv = LAST_VECTOR if e == E - 1 else W1_VECTOR[e % 2]
             interleave_permuted(nc.vector.tensor_copy, w1g, w1raw, 0, mv)
             interleave_permuted(nc.scalar.copy, w1g, w1raw, mv, P)
             w1gs[e] = w1g
@@ -124,23 +123,19 @@ def tile_routed_moe_kernel(tc, xT, w1, w2, gate, offs, pos1, pos2, out):
             )
             w1codes[e] = (w1q, w1s)
 
-        def weights2(e, stage):
+        def group2(e, stage):
             w2raw = w2raws[e]
             w2g = in_mid([P, N, PACK], f"w2g{e}", stage)
-            nc.gpsimd.tensor_scalar(
-                out=w2g[:],
-                in0=w2raw.rearrange("p j n -> p n j"),
-                scalar1=1.0,
-                scalar2=0.0,
-                op0=MULT,
-                op1=ADD,
-            )
+            interleave(nc.vector.tensor_copy, w2g, w2raw)
+            w2gs[e] = w2g
+
+        def quantise2(e):
             w2q = wq.tile([P, N], U32, name="w2q", tag="w2q", align_bytes=64)
             w2s = wq.tile([P, N], U8, name="w2s", tag="w2s", align_bytes=64)
             nc.vector.quantize_mx(
                 out=w2q[:].bitcast(FP8X4),
                 scales=w2s[:],
-                in_=w2g[:].rearrange("p n j -> p (n j)"),
+                in_=w2gs[e][:].rearrange("p n j -> p (n j)"),
             )
             w2codes[e] = (w2q, w2s)
 
@@ -221,10 +216,13 @@ def tile_routed_moe_kernel(tc, xT, w1, w2, gate, offs, pos1, pos2, out):
             if e >= 4:
                 load(e + RING - 4)
             quantise1(e)
+            if e >= 1:
+                group2(e - 1, e)
             gather(e % 2, e + 2 - e % 2, e)
             if e >= 1:
-                weights2(e - 1, e)
-        weights2(E - 1, E)
+                quantise2(e - 1)
+        group2(E - 1, E)
+        quantise2(E - 1)
         layer1(E - 1, None)
         layer2(E - 2, None)
         layer2(E - 1, None)
@@ -237,7 +235,7 @@ def tile_routed_moe_kernel(tc, xT, w1, w2, gate, offs, pos1, pos2, out):
             t0, width = OUT_CHUNKS[c]
             parts = []
             for r, pos in ((0, pos1_sb), (1, pos2_sb)):
-                part = fin.tile([P, width], F32, name="part", tag=f"part{r}")
+                part = fin.tile([P, width], F32, name="part", tag=f"part{r}", bufs=3)
                 nc.vector.tensor_tensor(
                     out=part[:],
                     in0=y_all[:].indirect(pos[:, t0 // 16 : (t0 + width) // 16]),
@@ -253,9 +251,5 @@ def tile_routed_moe_kernel(tc, xT, w1, w2, gate, offs, pos1, pos2, out):
             nc.vector.tensor_add(out=total[:], in0=parts[0][:], in1=parts[1][:])
             nc.sync.dma_start(out=out[:, t0 : t0 + width], in_=total[:])
 
-        fetched = fetch(0)
-        for c in range(1, len(OUT_CHUNKS)):
-            following = fetch(c)
-            finish(c - 1, fetched)
-            fetched = following
-        finish(len(OUT_CHUNKS) - 1, fetched)
+        for c in range(len(OUT_CHUNKS)):
+            finish(c, fetch(c))

from contextlib import ExitStack

import concourse.mybir as mybir

K, T, E, C, H, N = 512, 1536, 12, 256, 512, 128
P = 128
PACK = 4
SLOTS = E * C
FLOPS = 2 * SLOTS * (K * H + H * N)

F32 = mybir.dt.float32
BF16 = mybir.dt.bfloat16
U32 = mybir.dt.uint32
U16 = mybir.dt.uint16
U8 = mybir.dt.uint8
FP8X4 = mybir.dt.float8_e4m3fn_x4
MULT = mybir.AluOpType.mult
RELU = mybir.ActivationFunctionType.Relu

X_CHUNKS = ((0, 512, 320), (512, 512, 320), (1024, 256, 160), (1280, 256, 160))
W1_VECTOR = (40, 48)
LAST_VECTOR = 72
VECTOR_RELU = ((11, 1),)
OUT_CHUNKS = ((0, 640), (640, 576), (1216, 320))
RING = 8
SLOT = PACK * H * 4
AT_HG, AT_HQ, AT_HS, AT_GQ, AT_GS = 0, 2048, 3072, 3328, 5376
GROUPED = PACK * H * 2


def interleave(copy, dst, src):
    copy(
        out=dst.rearrange("p (c i) j -> p c j i", i=4),
        in_=src.rearrange("p j (c i) -> p c j i", i=4),
    )


def interleave_permuted(copy, dst, src, m0, m1):
    copy(
        out=dst[:, :, m0:m1, :].rearrange("p t m j -> p m j t"),
        in_=src[:, :, 4 * m0 : 4 * m1].rearrange("p j (m t) -> p m j t", t=4),
    )


def tile_routed_moe_kernel(tc, xT, w1, w2, gate, offs, pos1, pos2, out):
    nc = tc.nc
    with ExitStack() as ctx:
        keep = ctx.enter_context(tc.tile_pool(name="keep", bufs=1))
        ring = ctx.enter_context(tc.tile_pool(name="ring", bufs=1))
        mid = ctx.enter_context(tc.tile_pool(name="mid", bufs=1))
        xin = ctx.enter_context(tc.tile_pool(name="xin", bufs=4))
        win = ctx.enter_context(tc.tile_pool(name="win", bufs=3))
        wq = ctx.enter_context(tc.tile_pool(name="wq", bufs=4))
        fin = ctx.enter_context(tc.tile_pool(name="fin", bufs=2))
        hps = ctx.enter_context(tc.psum_pool(name="hps", bufs=5))
        yps = ctx.enter_context(tc.psum_pool(name="yps", bufs=3))

        offs_sb = keep.tile([P, SLOTS // 16], U16, name="offs_sb")
        pos1_sb = keep.tile([P, T // 16], U16, name="pos1_sb")
        pos2_sb = keep.tile([P, T // 16], U16, name="pos2_sb")
        xq = keep.tile([P, T], U32, name="xq", align_bytes=64)
        xs = keep.tile([P, T], U8, name="xs", align_bytes=64)
        y_all = keep.tile([P, SLOTS], F32, name="y_all")
        gate_sb = keep.tile([P, 2, T], F32, name="gate_sb")

        nc.gpsimd.memset(xs[:], 0)

        x_view = xT.rearrange("(p j) n -> p j n", j=PACK)
        w2raws, w1raws, w1gs, w2codes, w1codes, words, scales, hgs, w2gs = {}, {}, {}, {}, {}, {}, {}, {}, {}

        def in_ring(shape, dtype, name, stage, at):
            if stage is None:
                return keep.tile(shape, dtype, name=name, align_bytes=64)
            return ring.tile(shape, dtype, name=name, align_bytes=64, offset=(stage % RING) * SLOT + at)

        def in_mid(shape, name, stage):
            return mid.tile(shape, BF16, name=name, align_bytes=64, offset=(stage % 3) * GROUPED)

        def tokens(c):
            n0, width, cut = X_CHUNKS[c]
            raw = xin.tile([P, PACK, width], F32, name="xraw", tag="xraw")
            nc.sync.dma_start(out=raw[:], in_=x_view[:, :, n0 : n0 + width])
            grouped = xin.tile([P, width, PACK], BF16, name="xg", tag="xg", align_bytes=64)
            interleave(nc.vector.tensor_copy, grouped[:, :cut, :], raw[:, :, :cut])
            if cut < width:
                interleave(nc.scalar.copy, grouped[:, cut:, :], raw[:, :, cut:])
            nc.vector.quantize_mx(
                out=xq[:, n0 : n0 + width].bitcast(FP8X4),
                scales=xs[:, n0 : n0 + width],
                in_=grouped[:].rearrange("p n j -> p (n j)"),
            )

        def load(e):
            if e >= E:
                return
            w1raw = in_ring([P, PACK, H], F32, f"w1raw{e}", e, 0)
            nc.sync.dma_start(out=w1raw[:], in_=w1[e].rearrange("(p j) c -> p j c", j=PACK))
            w1raws[e] = w1raw
            if e % 2 == 1:
                w2raw = win.tile([P, 2, PACK, N], F32, name="w2raw", tag="w2raw")
                nc.sync.dma_start(
                    out=w2raw[:],
                    in_=w2[e - 1 : e + 1].rearrange("e (p j) n -> p e j n", j=PACK),
                )
                w2raws[e - 1] = w2raw[:, 0]
                w2raws[e] = w2raw[:, 1]

        def group1(e):
            w1raw = w1raws[e]
            w1g = in_mid([P, PACK, P, PACK], f"w1g{e}", e)
            mv = LAST_VECTOR if e == E - 1 else W1_VECTOR[e % 2]
            interleave_permuted(nc.vector.tensor_copy, w1g, w1raw, 0, mv)
            interleave_permuted(nc.scalar.copy, w1g, w1raw, mv, P)
            w1gs[e] = w1g

        def quantise1(e):
            w1q = wq.tile([P, H], U32, name="w1q", tag="w1q", align_bytes=64)
            w1s = wq.tile([P, H], U8, name="w1s", tag="w1s", align_bytes=64)
            nc.vector.quantize_mx(
                out=w1q[:].bitcast(FP8X4),
                scales=w1s[:],
                in_=w1gs[e][:].rearrange("p t m j -> p (t m j)"),
            )
            w1codes[e] = (w1q, w1s)

        def group2(e, stage):
            w2raw = w2raws[e]
            w2g = in_mid([P, N, PACK], f"w2g{e}", stage)
            interleave(nc.vector.tensor_copy, w2g, w2raw)
            w2gs[e] = w2g

        def quantise2(e):
            w2q = wq.tile([P, N], U32, name="w2q", tag="w2q", align_bytes=64)
            w2s = wq.tile([P, N], U8, name="w2s", tag="w2s", align_bytes=64)
            nc.vector.quantize_mx(
                out=w2q[:].bitcast(FP8X4),
                scales=w2s[:],
                in_=w2gs[e][:].rearrange("p n j -> p (n j)"),
            )
            w2codes[e] = (w2q, w2s)

        def gather(sort, e, stage):
            if e >= E:
                return
            picked = offs_sb[:, e * C // 16 : (e + 2) * C // 16]
            if sort == 0:
                gq = in_ring([P, 2 * C], U32, f"gq{e}", stage, AT_GQ)
                nc.vector.tensor_copy(out=gq[:], in_=xq[:].indirect(picked))
                words[e] = gq
            else:
                gs = in_ring([P, 2 * C], U8, f"gs{e}", stage, AT_GS)
                nc.vector.tensor_copy(out=gs[:], in_=xs[:].indirect(picked))
                scales[e] = gs

        def layer1(e, stage):
            w1q, w1s = w1codes[e]
            gq, gs = words[e - e % 2], scales[e - e % 2]
            hg = in_ring([P, C, PACK], BF16, f"hg{e}", stage, AT_HG)
            for half in range(2):
                n0 = e % 2 * C + half * P
                hp = hps.tile([P, PACK, P], F32, name="hp", tag="hp")
                for t in range(PACK):
                    nc.tensor.matmul_mx(
                        out=hp[:, t, :],
                        lhsT=w1q[:, t * P : (t + 1) * P].bitcast(FP8X4),
                        lhsT_scale=w1s[:, t * P : (t + 1) * P],
                        rhs=gq[:, n0 : n0 + P].bitcast(FP8X4),
                        rhs_scale=gs[:, n0 : n0 + P],
                        start=True,
                        stop=True,
                    )
                hidden = hg[:, half * P : (half + 1) * P, :]
                sums = hp[:].rearrange("p t n -> p n t")
                if (e, half) in VECTOR_RELU:
                    nc.vector.tensor_scalar_max(hidden, sums, 0.0)
                else:
                    nc.scalar.activation(out=hidden, in_=sums, func=RELU)
            hgs[e] = hg

        def layer2(e, stage):
            hq = in_ring([P, C], U32, f"hq{e}", stage, AT_HQ)
            hs = in_ring([P, C], U8, f"hs{e}", stage, AT_HS)
            nc.vector.quantize_mx(
                out=hq[:].bitcast(FP8X4),
                scales=hs[:],
                in_=hgs[e][:].rearrange("p n t -> p (n t)"),
            )
            yp = yps.tile([P, C], F32, name="yp", tag="yp")
            w2q, w2s = w2codes[e]
            nc.tensor.matmul_mx(
                out=yp[:],
                lhsT=w2q[:].bitcast(FP8X4),
                lhsT_scale=w2s[:],
                rhs=hq[:].bitcast(FP8X4),
                rhs_scale=hs[:],
                start=True,
                stop=True,
            )
            nc.scalar.copy(out=y_all[:, e * C : (e + 1) * C], in_=yp[:])

        tokens(0)
        tokens(1)
        nc.sync.dma_start(offs_sb[:], offs)
        for c in range(2, len(X_CHUNKS)):
            tokens(c)
        for e in range(RING):
            load(e)
        gather(0, 0, None)
        gather(1, 0, None)
        for e in range(E):
            group1(e)
            if e >= 1:
                layer1(e - 1, e)
            if e >= 2:
                layer2(e - 2, e)
            if e >= 4:
                load(e + RING - 4)
            quantise1(e)
            if e >= 1:
                group2(e - 1, e)
            gather(e % 2, e + 2 - e % 2, e)
            if e >= 1:
                quantise2(e - 1)
        group2(E - 1, E)
        quantise2(E - 1)
        layer1(E - 1, None)
        layer2(E - 2, None)
        layer2(E - 1, None)

        nc.sync.dma_start(pos1_sb[:], pos1)
        nc.sync.dma_start(pos2_sb[:], pos2)
        nc.sync.dma_start(out=gate_sb[:], in_=gate.rearrange("g p t -> p g t"))

        def fetch(c):
            t0, width = OUT_CHUNKS[c]
            parts = []
            for r, pos in ((0, pos1_sb), (1, pos2_sb)):
                part = fin.tile([P, width], F32, name="part", tag=f"part{r}", bufs=3)
                nc.vector.tensor_tensor(
                    out=part[:],
                    in0=y_all[:].indirect(pos[:, t0 // 16 : (t0 + width) // 16]),
                    in1=gate_sb[:, r, t0 : t0 + width],
                    op=MULT,
                )
                parts.append(part)
            return parts

        def finish(c, parts):
            t0, width = OUT_CHUNKS[c]
            total = fin.tile([P, width], F32, name="total", tag="total")
            nc.vector.tensor_add(out=total[:], in0=parts[0][:], in1=parts[1][:])
            nc.sync.dma_start(out=out[:, t0 : t0 + width], in_=total[:])

        for c in range(len(OUT_CHUNKS)):
            finish(c, fetch(c))
